import numpy as np
import ml_dtypes


def mxq(x, axis, fmt="e4m3"):
    dtype, down = {"e4m3": (ml_dtypes.float8_e4m3fn, 7), "e5m2": (ml_dtypes.float8_e5m2, 14)}[fmt]
    v = np.moveaxis(np.asarray(x, np.float32).astype(ml_dtypes.bfloat16).astype(np.float64), axis, -1)
    blocks = v.reshape(v.shape[:-1] + (-1, 32))
    amax = np.abs(blocks).max(-1, keepdims=True)
    byte = np.maximum(np.where(amax > 0, np.frexp(amax)[1] - 1 + 127, 0) - down, 1)
    scale = np.exp2(byte - 127.0)
    codes = (blocks / scale).astype(np.float32).astype(dtype).astype(np.float64)
    return np.moveaxis((codes * scale).reshape(v.shape), -1, axis)


WIDE = False


def mx_kscale(k):
    if not WIDE:
        return np.ones(k)
    levels = np.array([10, -10, 5, -5, 0])
    if k % 512:
        return np.exp2(np.random.permutation(np.resize(levels, k // 32))).repeat(32)
    a = np.empty((k // 512, 16))
    for p in range(k // 512):
        a[p, :8] = np.random.permutation(np.resize(levels, 8))
        for g in range(8):
            far = levels[np.abs(levels - a[p, g]) >= 10]
            a[p, g + 8] = far[np.random.randint(len(far))]
    return np.exp2(a.ravel()).repeat(32)


BF16 = ml_dtypes.bfloat16


def bf(x):
    return np.asarray(x, np.float32).astype(BF16)


def f64(x):
    return np.asarray(x).astype(np.float64)


E2M1 = np.array([0.0, 0.5, 1.0, 1.5, 2.0, 3.0, 4.0, 6.0, -0.0, -0.5, -1.0, -1.5, -2.0, -3.0, -4.0, -6.0])


def pack_weight(w, fmt):
    k, n = w.shape
    w = f64(bf(w)).reshape(k // 32, 32, n)
    amax = np.abs(w).max(1)
    if fmt == "e4m3":
        byte = np.frexp(amax)[1] - 1 + 127 - 7
    else:
        mant, ex = np.frexp(amax / 6.0)
        byte = np.where(mant > 0.5, ex, ex - 1) + 127
    byte = np.clip(np.where(amax > 0, byte, 1), 1, 254)
    scaled = (w * np.exp2(127.0 - byte)[:, None, :]).reshape(k, n).astype(np.float32)
    by_word = np.ascontiguousarray(scaled.reshape(k // 512, 128, 4, n).transpose(0, 1, 3, 2))
    if fmt == "e4m3":
        words = by_word.astype(ml_dtypes.float8_e4m3fn).view(np.uint8)
    else:
        c = by_word.astype(ml_dtypes.float4_e2m1fn).view(np.uint8) & 0xF
        words = c[..., 0::2] | (c[..., 1::2] << 4)
    return np.ascontiguousarray(words), np.ascontiguousarray(byte.astype(np.uint8).reshape(k // 512, 16, n))


def unpack_weight(words, scales, fmt):
    g, p, n, _ = words.shape
    if fmt == "e4m3":
        vals = np.ascontiguousarray(words).view(ml_dtypes.float8_e4m3fn).astype(np.float64)
    else:
        nib = np.empty((g, p, n, 4), np.uint8)
        nib[..., 0::2] = words & 0xF
        nib[..., 1::2] = words >> 4
        vals = E2M1[nib]
    vals = vals * np.repeat(np.exp2(scales.astype(np.float64) - 127.0), 8, axis=1)[..., None]
    return vals.transpose(0, 1, 3, 2).reshape(g * 512, n)
def pack4(w):
    words, scales = pack_weight(w, "e2m1")
    return words.reshape(words.shape[0], 128, -1), scales


def unpack4(words, scales):
    return unpack_weight(words.reshape(words.shape[0], 128, -1, 2), scales, "e2m1")


def planes(Y):
    n, m = Y.shape
    b = f64(bf(Y)).reshape(n // 32, 32, m)
    amax = np.abs(b).max(1)
    byte = np.clip(np.where(amax > 0, np.frexp(amax)[1] - 1 + 127 - 7, 1), 1, 254)
    codes = (b * np.exp2(127.0 - byte)[:, None, :]).reshape(n, m).astype(np.float32).astype(ml_dtypes.float8_e4m3fn).view(np.uint8)
    words = codes.reshape(n // 512, 128, 4, m).transpose(0, 1, 3, 2)
    return np.ascontiguousarray(words), np.ascontiguousarray(byte.astype(np.uint8).reshape(n // 512, 16, m))


J, L, N, D = 128, 16, 512, 1024


def setup_inputs():
    a, t = mx_kscale(N), mx_kscale(D)
    level = np.random.uniform(0.5, 2.0, (J, 1, 1))
    s = bf(np.random.standard_normal((J, L, N)) * level * a)
    ydec_words, ydec_scales = pack4(np.random.standard_normal((N, D)) / np.sqrt(N) / a[:, None])
    thr = bf(np.random.uniform(0.2, 2.0, D))
    w = bf((1.0 + 0.1 * np.random.standard_normal(D)) * t)
    yenc_words, yenc_scales = pack4(np.random.standard_normal((D, N)) / np.sqrt(D) / t[:, None])
    return {"s": s,
            "ydec_words": ydec_words,
            "ydec_scales": ydec_scales,
            "thr": thr,
            "w": w,
            "yenc_words": yenc_words,
            "yenc_scales": yenc_scales}


def block_energy(d):
    return np.mean(np.square(d), axis=1)


def compressor_gain(e, thr):
    return np.power(1.0 + e / thr[None, :], -0.35)


def core(s, ydec_words, ydec_scales, thr, w, yenc_words, yenc_scales):
    d = mxq(f64(s), 2, "e4m3") @ unpack4(ydec_words, ydec_scales)
    e = block_energy(d)
    q = compressor_gain(e, f64(thr))
    c = d * q[:, None, :] * f64(w)[None, None, :]
    return mxq(c, 2, "e4m3") @ unpack4(yenc_words, yenc_scales)


def reference(s, ydec_words, ydec_scales, thr, w, yenc_words, yenc_scales):
    R_out = core(s, ydec_words, ydec_scales, thr, w, yenc_words, yenc_scales)
    words, scales = planes(np.moveaxis(R_out, 2, 0).reshape(512, -1))
    return R_out, words, scales

@@ -1,0 +1,396 @@
+from contextlib import ExitStack
+
+import concourse.mybir as mybir
+from concourse.masks import make_identity
+
+TOKENS, CH, DIRS = 2048, 512, 1024
+SAMPLES = 16
+BLOCKS = TOKENS // SAMPLES
+P = 128
+FLOPS = 2 * TOKENS * CH * DIRS * 2
+
+F32 = mybir.dt.float32
+BF16 = mybir.dt.bfloat16
+I32 = mybir.dt.int32
+U32 = mybir.dt.uint32
+U8 = mybir.dt.uint8
+FP8X4 = mybir.dt.float8_e4m3fn_x4
+FP4X4 = mybir.dt.float4_e2m1fn_x4
+ACT = mybir.ActivationFunctionType
+ALU = mybir.AluOpType
+AX = mybir.AxisListType
+
+UNITS = [(0, 128), (128, 128), (256, 256), (512, 512), (1024, 512), (1536, 512)]
+NT = TOKENS // P
+FOLDED = (0, 1, 2, 3, 4, 5, 6, 8, 9, 10, 12, 13)
+LAG = 2
+DIRECT = (14, 15)
+
+
+def tile_ambisonicdirectionaldynamicrangecompress_x2_kernel(
+    tc, s, ydec_words, ydec_scales, thr, w, yenc_words, yenc_scales, out_0, out_1, out_2
+):
+    nc = tc.nc
+    s_rows = s.rearrange("j l n -> (j l) n")
+    out_rows = out_0.rearrange("j l n -> (j l) n")
+    word_rows = out_1[0].rearrange("p m t -> p (m t)").bitcast(I32)
+    scale_rows = out_2[0].bitcast(I32)
+
+    with ExitStack() as ctx:
+        keep = ctx.enter_context(tc.tile_pool(name="keep", bufs=1))
+        work = ctx.enter_context(tc.tile_pool(name="work", bufs=3))
+        psum = ctx.enter_context(tc.psum_pool(name="psum", bufs=6))
+        ctx.enter_context(tc.manual_schedule())
+
+        ident = keep.tile([P, P], F32, name="ident")
+        make_identity(nc, ident[:])
+
+        yd_raw = keep.tile([P, 2 * DIRS], U8, name="yd_raw", align_bytes=64)
+        ys_raw = keep.tile([P, DIRS], U8, name="ys_raw", align_bytes=64)
+        yd = keep.tile([P, 2, 4, P, 2], U8, name="yd", align_bytes=64)
+        ys = keep.tile([P, 2, 4, P], U8, name="ys", align_bytes=64)
+        ye = keep.tile([P, 2, 2 * CH], U8, name="ye", align_bytes=64)
+        yes = keep.tile([P, 2, CH], U8, name="yes", align_bytes=64)
+        yp = keep.tile([P, 2, 4, P, 2], U8, name="yp", align_bytes=64)
+        yps = keep.tile([P, 2, 4, P], U8, name="yps", align_bytes=64)
+        thr_b = keep.tile([P, 2, 4], BF16, name="thr_b")
+        w_b = keep.tile([P, 2, 4], BF16, name="w_b")
+        thr16 = keep.tile([P, 8], F32, name="thr16")
+        lnthr = keep.tile([P, 8], F32, name="lnthr")
+        powthr = keep.tile([P, 8], F32, name="powthr")
+        wq = keep.tile([P, 2, 4], F32, name="wq")
+
+        nc.vector.memset(ys_raw[:].bitcast(I32), 0)
+        nc.vector.memset(yes[:].rearrange("p g n -> p (g n)").bitcast(I32), 0)
+
+        x_tiles = []
+        for tok, width in UNITS:
+            x = keep.tile([P, width // P, CH], BF16, name="x%d" % tok)
+            x_tiles.append(x)
+
+        def load_x(u):
+            tok, width = UNITS[u]
+            nc.sync.dma_start(out=x_tiles[u][:], in_=s_rows[tok : tok + width, :].rearrange("(i p) n -> p i n", p=P))
+
+        load_x(0)
+        nc.sync.dma_start(out=yd_raw[:].bitcast(I32), in_=ydec_words[0].bitcast(I32))
+        for q in range(4):
+            nc.scalar.dma_start(out=ys_raw[32 * q : 32 * q + 4, :].bitcast(I32), in_=ydec_scales[0, 4 * q : 4 * q + 4, :].bitcast(I32))
+        nc.scalar.dma_start(out=thr_b[:], in_=thr.rearrange("(g p t) -> p g t", g=2, t=4))
+        nc.scalar.dma_start(out=w_b[:], in_=w.rearrange("(g p t) -> p g t", g=2, t=4))
+        for u in range(1, len(UNITS)):
+            load_x(u)
+        nc.sync.dma_start(out=ye[:].rearrange("p g n -> p (g n)").bitcast(I32).rearrange("p (g n) -> p g n", g=2), in_=yenc_words.rearrange("g p n -> p g n").bitcast(I32))
+        for q in range(4):
+            nc.sync.dma_start(
+                out=yes[32 * q : 32 * q + 4, :, :].rearrange("p g n -> p (g n)").bitcast(I32).rearrange("p (g n) -> p g n", g=2),
+                in_=yenc_scales[:, 4 * q : 4 * q + 4, :].rearrange("g q n -> q g n").bitcast(I32),
+            )
+
+        nc.scalar.activation(out=lnthr[:], in_=thr_b[:].rearrange("p g t -> p (g t)"), func=ACT.Ln, scale=16.0)
+
+        s_codes = keep.tile([P, TOKENS], U32, name="s_codes", align_bytes=64)
+        s_scales = keep.tile([P, TOKENS], U8, name="s_scales", align_bytes=64)
+        energy = keep.tile([P, 8, BLOCKS], F32, name="energy")
+        lnsum = keep.tile([P, 8, BLOCKS], F32, name="lnsum")
+        power = keep.tile([P, 8, BLOCKS], F32, name="power")
+        gain = keep.tile([P, 2, BLOCKS, 4], F32, name="gain")
+
+        def permute_ydec(g):
+            nc.vector.tensor_copy(
+                out=yd[:, g],
+                in_=yd_raw[:, 1024 * g : 1024 * (g + 1)].rearrange("p (m t b) -> p t m b", t=4, b=2),
+            )
+            nc.vector.tensor_copy(
+                out=ys[:, g],
+                in_=ys_raw[:, 512 * g : 512 * (g + 1)].rearrange("p (m t) -> p t m", t=4),
+            )
+
+        def permute_yenc():
+            for g in range(2):
+                nc.vector.tensor_copy(out=yp[:, g], in_=ye[:, g].rearrange("p (m t b) -> p t m b", t=4, b=2))
+            nc.vector.tensor_copy(out=yps[:], in_=yes[:].rearrange("p g (m t) -> p g t m", t=4))
+
+        xg_tiles = {}
+
+        def turn(u, b, scalar=False):
+            tok, width = UNITS[u]
+            if u not in xg_tiles:
+                xg = work.tile([P, 512, 4], BF16, name="xg", align_bytes=64)
+                xg_tiles[u] = xg
+            n = min(256, width - b)
+            xt = psum.tile([P, 2, 2, P], F32, name="xt", bufs=2)
+            for i in range(n // P):
+                words = x_tiles[u][:, b // P + i, :].bitcast(F32)
+                for h in range(2):
+                    nc.tensor.transpose(xt[:, i, h, :], words[:, h::2], ident[:])
+            (nc.scalar.copy if scalar else nc.vector.tensor_copy)(
+                out=xg_tiles[u][:, b : b + n, :].rearrange("p n t -> p (n t)").bitcast(F32).rearrange("p (i r h) -> p i r h", h=2, r=P),
+                in_=xt[:, : n // P].rearrange("p i h r -> p i r h"),
+            )
+
+        def quant_s(u):
+            tok, width = UNITS[u]
+            nc.vector.quantize_mx(
+                out=s_codes[:, tok : tok + width].bitcast(FP8X4),
+                scales=s_scales[:, tok : tok + width],
+                in_=xg_tiles.pop(u)[:, :width, :].rearrange("p n t -> p (n t)"),
+            )
+
+        def decode(out, g, t, tok, width):
+            nc.tensor.matmul_mx(
+                out=out,
+                lhsT=yd[:, g, t].rearrange("p m b -> p (m b)").bitcast(FP4X4),
+                lhsT_scale=ys[:, g, t],
+                rhs=s_codes[:, tok : tok + width].bitcast(FP8X4),
+                rhs_scale=s_scales[:, tok : tok + width],
+                start=True,
+                stop=True,
+            )
+
+        pairs = [(u, k) for u in range(len(UNITS)) for k in range(UNITS[u][1] // P)]
+        N_PAIRS = len(pairs)
+        squares = {}
+
+        def square(n):
+            u, pair = pairs[n]
+            tok, width = UNITS[u]
+            per_bank = 512 // width
+            sq = work.tile([P, 2, 512], F32, name="sq", bufs=5)
+            for half in range(2):
+                bank = psum.tile([P, 512], F32, name="acc")
+                d0 = (2 * pair + half) * per_bank
+                for k in range(per_bank):
+                    decode(bank[:, k * width : (k + 1) * width], (d0 + k) // 4, (d0 + k) % 4, tok, width)
+                nc.scalar.activation(out=sq[:, half], in_=bank[:], func=ACT.Square)
+            squares[n] = sq
+            if n in FOLDED:
+                fold = work.tile([P, 64, 8], F32, name="fold", bufs=4)
+                v = sq[:].rearrange("p h (b l) -> p (h b) l", l=SAMPLES)
+                nc.gpsimd.tensor_tensor(out=fold[:], in0=v[:, :, 0:8], in1=v[:, :, 8:16], op=ALU.add)
+                squares[n] = fold
+
+        def sums(n):
+            u, pair = pairs[n]
+            tok, width = UNITS[u]
+            per_bank = 512 // width
+            nb = width // SAMPLES
+            t = squares.pop(n)
+            d0 = 2 * pair * per_bank
+            blocks = slice(tok // SAMPLES, tok // SAMPLES + nb)
+            if n in FOLDED:
+                nc.vector.tensor_reduce(
+                    out=energy[:, d0 : d0 + 2 * per_bank, blocks],
+                    in_=t[:].rearrange("p (d b) l -> p d b l", b=nb),
+                    axis=AX.X,
+                    op=ALU.add,
+                )
+            else:
+                for half in range(2):
+                    nc.vector.tensor_reduce(
+                        out=energy[:, d0 + half * per_bank : d0 + (half + 1) * per_bank, blocks],
+                        in_=t[:, half].rearrange("p (d b l) -> p d b l", b=nb, l=SAMPLES),
+                        axis=AX.X,
+                        op=ALU.add,
+                    )
+
+        def log_gain(b0, b1, k0=0, k1=8):
+            for k in range(k0, k1):
+                nc.scalar.activation(out=lnsum[:, k, b0:b1], in_=energy[:, k, b0:b1], func=ACT.Ln, bias=thr16[:, k : k + 1])
+
+        turn(0, 0)
+        quant_s(0)
+        permute_ydec(0)
+        turn(1, 0, True)
+        permute_ydec(1)
+        quant_s(1)
+        nc.vector.tensor_scalar(thr16[:], thr_b[:].rearrange("p g t -> p (g t)"), 16.0, None, ALU.mult)
+        done = 0
+        for n in range(N_PAIRS):
+            square(n)
+            u, pair = pairs[n]
+            if n == 0:
+                turn(2, 0, True)
+                quant_s(2)
+            if n == 1:
+                turn(3, 0)
+            if n == 2:
+                turn(3, 256)
+                quant_s(3)
+            if u in (3, 4):
+                if pair == 0:
+                    turn(u + 1, 0)
+                if pair == 1:
+                    turn(u + 1, 256)
+                if pair == 2:
+                    quant_s(u + 1)
+            while done <= n - LAG:
+                sums(done)
+                done += 1
+        while done < N_PAIRS:
+            sums(done)
+            done += 1
+        log_gain(0, BLOCKS)
+        permute_yenc()
+
+        def finish_gain(b0, b1, first):
+            nc.scalar.activation(out=power[:, :, b0:b1], in_=lnsum[:, :, b0:b1], func=ACT.Exp, scale=-0.35)
+            eng = nc.vector if first else nc.gpsimd
+            eng.tensor_tensor(
+                out=gain[:, :, b0:b1, :],
+                in0=power[:, :, b0:b1].rearrange("p (g t) b -> p g b t", g=2),
+                in1=wq[:].unsqueeze(2).to_broadcast([P, 2, b1 - b0, 4]),
+                op=ALU.mult,
+            )
+
+        nc.scalar.activation(out=powthr[:], in_=lnthr[:], func=ACT.Exp, scale=0.35)
+        nc.vector.tensor_tensor(out=wq[:].rearrange("p g t -> p (g t)"), in0=powthr[:], in1=w_b[:].rearrange("p g t -> p (g t)"), op=ALU.mult)
+        finish_gain(0, 8, True)
+        finish_gain(8, 32, False)
+        finish_gain(32, 80, False)
+        finish_gain(80, 128, False)
+
+        p_codes = keep.tile([P, TOKENS], U32, name="p_codes", align_bytes=64)
+        p_scales = keep.tile([P, TOKENS], U8, name="p_scales", align_bytes=64)
+        banks = {}
+        comp = {}
+        ccodes = {}
+        rounded = {}
+        turned = {}
+        direct = {}
+        results = {}
+
+        def stage1(i):
+            for g in range(2):
+                bank = psum.tile([P, 4, P], F32, name="acc")
+                for t in range(4):
+                    decode(bank[:, t], g, t, P * i, P)
+                banks[i, g] = bank
+
+        def apply_gain(i, g):
+            if g == 0:
+                c = work.tile([P, 2, P, 4], BF16, name="c", align_bytes=64)
+                comp[i] = c
+            nc.vector.tensor_tensor(
+                out=comp[i][:, g].rearrange("p (b l) t -> p b l t", l=SAMPLES),
+                in0=banks.pop((i, g))[:].rearrange("p t (b l) -> p b l t", l=SAMPLES),
+                in1=gain[:, g, 8 * i : 8 * i + 8, :].unsqueeze(2).to_broadcast([P, 8, SAMPLES, 4]),
+                op=ALU.mult,
+            )
+
+        def quant_c(i):
+            cw = work.tile([P, 2, P], U32, name="cw", align_bytes=64)
+            cs = work.tile([P, 2, P], U8, name="cs", align_bytes=64)
+            nc.vector.quantize_mx(
+                out=cw[:].rearrange("p g n -> p (g n)").bitcast(FP8X4),
+                scales=cs[:].rearrange("p g n -> p (g n)"),
+                in_=comp.pop(i)[:].rearrange("p g n t -> p (g n t)"),
+            )
+            ccodes[i] = (cw, cs)
+
+        def stage2_planes(i):
+            cw, cs = ccodes[i]
+            bank = psum.tile([P, 4, P], F32, name="acc")
+            for t in range(4):
+                for g in range(2):
+                    nc.tensor.matmul_mx(
+                        out=bank[:, t],
+                        lhsT=yp[:, g, t].rearrange("p m b -> p (m b)").bitcast(FP4X4),
+                        lhsT_scale=yps[:, g, t],
+                        rhs=cw[:, g].bitcast(FP8X4),
+                        rhs_scale=cs[:, g],
+                        start=g == 0,
+                        stop=g == 1,
+                    )
+            direct[i] = bank
+
+        def copy_planes(i):
+            og = work.tile([P, 2 * P, 4], BF16, name="og", align_bytes=64)
+            nc.vector.tensor_copy(out=og[:, :P], in_=direct.pop(i)[:].rearrange("p t r -> p r t"))
+            turned[i] = og
+
+        def stage2(i):
+            cw, cs = ccodes.pop(i)
+            bank = psum.tile([P, CH], F32, name="acc")
+            for g in range(2):
+                nc.tensor.matmul_mx(
+                    out=bank[:],
+                    lhsT=cw[:, g].bitcast(FP8X4),
+                    lhsT_scale=cs[:, g],
+                    rhs=ye[:, g].bitcast(FP4X4),
+                    rhs_scale=yes[:, g],
+                    start=g == 0,
+                    stop=g == 1,
+                )
+            res = work.tile([P, CH], F32, name="res", bufs=4)
+            nc.scalar.copy(out=res[:], in_=bank[:])
+            nc.sync.dma_start(out=out_rows[P * i : P * (i + 1), :], in_=res[:])
+            if i not in DIRECT:
+                results[i] = res
+
+        def cast(i):
+            rb = work.tile([P, CH], BF16, name="rb", bufs=4)
+            nc.scalar.copy(out=rb[:], in_=results.pop(i)[:])
+            rounded[i] = rb
+
+        def turn_back(i):
+            xt = psum.tile([P, 2, 2, P], F32, name="xt", bufs=2)
+            for k in range(2):
+                words = rounded.pop(i + k)[:].bitcast(F32)
+                for h in range(2):
+                    nc.tensor.transpose(xt[:, k, h, :], words[:, h::2], ident[:])
+            og = work.tile([P, 2 * P, 4], BF16, name="og", align_bytes=64)
+            nc.scalar.copy(
+                out=og[:].rearrange("p n t -> p (n t)").bitcast(F32).rearrange("p (i r h) -> p i r h", h=2, r=P),
+                in_=xt[:].rearrange("p i h r -> p i r h"),
+            )
+            turned[i] = og
+
+        def quant_p(i, n):
+            cols = slice(P * i, P * (i + n))
+            nc.vector.quantize_mx(
+                out=p_codes[:, cols].bitcast(FP8X4),
+                scales=p_scales[:, cols],
+                in_=turned.pop(i)[:, : n * P].rearrange("p n t -> p (n t)"),
+            )
+            nc.sync.dma_start(out=word_rows[:, cols], in_=p_codes[:, cols].bitcast(I32))
+
+        def store_scales(i0, i1):
+            words = slice(i0 * P // 4, i1 * P // 4)
+            for q in range(4):
+                (nc.scalar if q % 2 else nc.sync).dma_start(
+                    out=scale_rows[4 * q : 4 * q + 4, words],
+                    in_=p_scales[32 * q : 32 * q + 4, :].bitcast(I32)[:, words],
+                )
+
+        stage1(0)
+        for i in range(NT):
+            if i + 1 < NT:
+                stage1(i + 1)
+            apply_gain(i, 0)
+            if i >= 1:
+                quant_c(i - 1)
+            apply_gain(i, 1)
+            if i - 1 in DIRECT:
+                stage2_planes(i - 1)
+            if i >= 1:
+                stage2(i - 1)
+            if i - 2 in results:
+                cast(i - 2)
+            if i % 2 == 0 and i - 4 in rounded:
+                turn_back(i - 4)
+            if i % 2 == 0 and i - 6 in turned:
+                quant_p(i - 6, 2)
+            if i == 14:
+                store_scales(0, 8)
+        quant_c(15)
+        stage2_planes(15)
+        stage2(15)
+        turn_back(12)
+        quant_p(10, 2)
+        copy_planes(14)
+        quant_p(14, 1)
+        copy_planes(15)
+        quant_p(12, 2)
+        quant_p(15, 1)
+        store_scales(8, NT)

@@ -22,9 +22,13 @@ AX = mybir.AxisListType
 
 UNITS = [(0, 128), (128, 128), (256, 256), (512, 512), (1024, 512), (1536, 512)]
 NT = TOKENS // P
-FOLDED = (0, 1, 2, 3, 4, 5, 6, 8, 9, 10, 12, 13)
+FOLDED = (2, 4, 5, 6, 8, 9, 10, 12, 13)
+TURN = {0: ((2, 0),), 1: ((3, 0), (3, 256)), 3: ((4, 0), (4, 256)), 5: ((5, 0), (5, 256))}
+ON_S = ()
+AFTER = {0: (("prep", 2),), 1: (("prep", 3), ("sum", 0)), 3: (("prep", 4), ("sum", 1)), 4: (("sum", 2), ("sum", 3)), 5: (("prep", 5), ("sum", 4)), 6: (("sum", 5),), 7: (("sum", 7),), 8: (("sum", 6),), 9: (), 10: (("sum", 8),), 11: (("sum", 9), ("sum", 11)), 12: (("sum", 10),), 13: (("sum", 12),), 14: (("sum", 14),), 15: (("sum", 13), ("sum", 15),)}
 LAG = 2
 DIRECT = (14, 15)
+ACC = 5
 
 
 def tile_ambisonicdirectionaldynamicrangecompress_x2_kernel(
@@ -39,7 +43,7 @@ def tile_ambisonicdirectionaldynamicrangecompress_x2_kernel(
     with ExitStack() as ctx:
         keep = ctx.enter_context(tc.tile_pool(name="keep", bufs=1))
         work = ctx.enter_context(tc.tile_pool(name="work", bufs=3))
-        psum = ctx.enter_context(tc.psum_pool(name="psum", bufs=6))
+        psum = ctx.enter_context(tc.psum_pool(name="psum", bufs=ACC))
         ctx.enter_context(tc.manual_schedule())
 
         ident = keep.tile([P, P], F32, name="ident")
@@ -73,9 +77,9 @@ def tile_ambisonicdirectionaldynamicrangecompress_x2_kernel(
             nc.sync.dma_start(out=x_tiles[u][:], in_=s_rows[tok : tok + width, :].rearrange("(i p) n -> p i n", p=P))
 
         load_x(0)
-        nc.sync.dma_start(out=yd_raw[:].bitcast(I32), in_=ydec_words[0].bitcast(I32))
         for q in range(4):
-            nc.scalar.dma_start(out=ys_raw[32 * q : 32 * q + 4, :].bitcast(I32), in_=ydec_scales[0, 4 * q : 4 * q + 4, :].bitcast(I32))
+            nc.sync.dma_start(out=ys_raw[32 * q : 32 * q + 4, :].bitcast(I32), in_=ydec_scales[0, 4 * q : 4 * q + 4, :].bitcast(I32))
+        nc.sync.dma_start(out=yd_raw[:].bitcast(I32), in_=ydec_words[0].bitcast(I32))
         nc.scalar.dma_start(out=thr_b[:], in_=thr.rearrange("(g p t) -> p g t", g=2, t=4))
         nc.scalar.dma_start(out=w_b[:], in_=w.rearrange("(g p t) -> p g t", g=2, t=4))
         for u in range(1, len(UNITS)):
@@ -113,20 +117,25 @@ def tile_ambisonicdirectionaldynamicrangecompress_x2_kernel(
 
         xg_tiles = {}
 
-        def turn(u, b, scalar=False):
-            tok, width = UNITS[u]
-            if u not in xg_tiles:
-                xg = work.tile([P, 512, 4], BF16, name="xg", align_bytes=64)
-                xg_tiles[u] = xg
-            n = min(256, width - b)
-            xt = psum.tile([P, 2, 2, P], F32, name="xt", bufs=2)
+        xt_tiles = {}
+
+        def turn(u, b):
+            n = min(256, UNITS[u][1] - b)
+            xt = psum.tile([P, 2, 2, P], F32, name="xt", bufs=8 - ACC)
             for i in range(n // P):
                 words = x_tiles[u][:, b // P + i, :].bitcast(F32)
                 for h in range(2):
                     nc.tensor.transpose(xt[:, i, h, :], words[:, h::2], ident[:])
-            (nc.scalar.copy if scalar else nc.vector.tensor_copy)(
+            xt_tiles[u, b] = xt
+
+        def spread(u, b, copy):
+            if b == 0:
+                xg = work.tile([P, 512, 4], BF16, name="xg", align_bytes=64)
+                xg_tiles[u] = xg
+            n = min(256, UNITS[u][1] - b)
+            copy(
                 out=xg_tiles[u][:, b : b + n, :].rearrange("p n t -> p (n t)").bitcast(F32).rearrange("p (i r h) -> p i r h", h=2, r=P),
-                in_=xt[:, : n // P].rearrange("p i h r -> p i r h"),
+                in_=xt_tiles.pop((u, b))[:, : n // P].rearrange("p i h r -> p i r h"),
             )
 
         def quant_s(u):
@@ -156,7 +165,7 @@ def tile_ambisonicdirectionaldynamicrangecompress_x2_kernel(
             u, pair = pairs[n]
             tok, width = UNITS[u]
             per_bank = 512 // width
-            sq = work.tile([P, 2, 512], F32, name="sq", bufs=5)
+            sq = work.tile([P, 2, 512], F32, name="sq", bufs=8)
             for half in range(2):
                 bank = psum.tile([P, 512], F32, name="acc")
                 d0 = (2 * pair + half) * per_bank
@@ -165,7 +174,7 @@ def tile_ambisonicdirectionaldynamicrangecompress_x2_kernel(
                 nc.scalar.activation(out=sq[:, half], in_=bank[:], func=ACT.Square)
             squares[n] = sq
             if n in FOLDED:
-                fold = work.tile([P, 64, 8], F32, name="fold", bufs=4)
+                fold = work.tile([P, 64, 8], F32, name="fold", bufs=6)
                 v = sq[:].rearrange("p h (b l) -> p (h b) l", l=SAMPLES)
                 nc.gpsimd.tensor_tensor(out=fold[:], in0=v[:, :, 0:8], in1=v[:, :, 8:16], op=ALU.add)
                 squares[n] = fold
@@ -198,38 +207,30 @@ def tile_ambisonicdirectionaldynamicrangecompress_x2_kernel(
             for k in range(k0, k1):
                 nc.scalar.activation(out=lnsum[:, k, b0:b1], in_=energy[:, k, b0:b1], func=ACT.Ln, bias=thr16[:, k : k + 1])
 
+        on_v = nc.vector.tensor_copy
+        on_s = nc.scalar.copy
+        on_v = nc.vector.tensor_copy
+        on_s = nc.scalar.copy
         turn(0, 0)
+        turn(1, 0)
+        spread(0, 0, on_v)
+        spread(1, 0, on_s)
         quant_s(0)
         permute_ydec(0)
-        turn(1, 0, True)
         permute_ydec(1)
         quant_s(1)
         nc.vector.tensor_scalar(thr16[:], thr_b[:].rearrange("p g t -> p (g t)"), 16.0, None, ALU.mult)
-        done = 0
         for n in range(N_PAIRS):
+            for u, b in TURN.get(n, ()):
+                turn(u, b)
             square(n)
-            u, pair = pairs[n]
-            if n == 0:
-                turn(2, 0, True)
-                quant_s(2)
-            if n == 1:
-                turn(3, 0)
-            if n == 2:
-                turn(3, 256)
-                quant_s(3)
-            if u in (3, 4):
-                if pair == 0:
-                    turn(u + 1, 0)
-                if pair == 1:
-                    turn(u + 1, 256)
-                if pair == 2:
-                    quant_s(u + 1)
-            while done <= n - LAG:
-                sums(done)
-                done += 1
-        while done < N_PAIRS:
-            sums(done)
-            done += 1
+            for kind, k in AFTER.get(n, ()):
+                if kind == "prep":
+                    for b in range(0, UNITS[k][1], 256):
+                        spread(k, b, on_s if (k, b) in ON_S else on_v)
+                    quant_s(k)
+                else:
+                    sums(k)
         log_gain(0, BLOCKS)
         permute_yenc()
 
@@ -260,12 +261,13 @@ def tile_ambisonicdirectionaldynamicrangecompress_x2_kernel(
         direct = {}
         results = {}
 
-        def stage1(i):
-            for g in range(2):
-                bank = psum.tile([P, 4, P], F32, name="acc")
-                for t in range(4):
-                    decode(bank[:, t], g, t, P * i, P)
-                banks[i, g] = bank
+        def stage1(i, g):
+            if i >= NT:
+                return
+            bank = psum.tile([P, 4, P], F32, name="acc")
+            for t in range(4):
+                decode(bank[:, t], g, t, P * i, P)
+            banks[i, g] = bank
 
         def apply_gain(i, g):
             if g == 0:
@@ -290,7 +292,7 @@ def tile_ambisonicdirectionaldynamicrangecompress_x2_kernel(
 
         def stage2_planes(i):
             cw, cs = ccodes[i]
-            bank = psum.tile([P, 4, P], F32, name="acc")
+            bank = psum.tile([P, 4, P], F32, name="o", tag="xt", bufs=8 - ACC)
             for t in range(4):
                 for g in range(2):
                     nc.tensor.matmul_mx(
@@ -311,7 +313,7 @@ def tile_ambisonicdirectionaldynamicrangecompress_x2_kernel(
 
         def stage2(i):
             cw, cs = ccodes.pop(i)
-            bank = psum.tile([P, CH], F32, name="acc")
+            bank = psum.tile([P, CH], F32, name="o", tag="xt", bufs=8 - ACC)
             for g in range(2):
                 nc.tensor.matmul_mx(
                     out=bank[:],
@@ -330,15 +332,18 @@ def tile_ambisonicdirectionaldynamicrangecompress_x2_kernel(
 
         def cast(i):
             rb = work.tile([P, CH], BF16, name="rb", bufs=4)
-            nc.scalar.copy(out=rb[:], in_=results.pop(i)[:])
+            nc.scalar.copy(
+                out=rb[:].rearrange("p (h w e) -> p h w e", h=2, e=2),
+                in_=results.pop(i)[:].rearrange("p (w h e) -> p h w e", h=2, e=2),
+            )
             rounded[i] = rb
 
         def turn_back(i):
-            xt = psum.tile([P, 2, 2, P], F32, name="xt", bufs=2)
+            xt = psum.tile([P, 2, 2, P], F32, name="xt", bufs=8 - ACC)
             for k in range(2):
                 words = rounded.pop(i + k)[:].bitcast(F32)
                 for h in range(2):
-                    nc.tensor.transpose(xt[:, k, h, :], words[:, h::2], ident[:])
+                    nc.tensor.transpose(xt[:, k, h, :], words[:, P * h : P * (h + 1)], ident[:])
             og = work.tile([P, 2 * P, 4], BF16, name="og", align_bytes=64)
             nc.scalar.copy(
                 out=og[:].rearrange("p n t -> p (n t)").bitcast(F32).rearrange("p (i r h) -> p i r h", h=2, r=P),
@@ -363,20 +368,27 @@ def tile_ambisonicdirectionaldynamicrangecompress_x2_kernel(
                     in_=p_scales[32 * q : 32 * q + 4, :].bitcast(I32)[:, words],
                 )
 
-        stage1(0)
+        for k in range(ACC):
+            stage1(k // 2, k % 2)
+        nxt = ACC
         for i in range(NT):
-            if i + 1 < NT:
-                stage1(i + 1)
             apply_gain(i, 0)
             if i >= 1:
                 quant_c(i - 1)
             apply_gain(i, 1)
+            if i == NT - 1:
+                turn_back(i - 3)
             if i - 1 in DIRECT:
                 stage2_planes(i - 1)
             if i >= 1:
                 stage2(i - 1)
+            for k in range(2):
+                stage1(nxt // 2, nxt % 2)
+                nxt += 1
             if i - 2 in results:
                 cast(i - 2)
+            if i == NT - 2:
+                cast(i - 1)
             if i % 2 == 0 and i - 4 in rounded:
                 turn_back(i - 4)
             if i % 2 == 0 and i - 6 in turned:
@@ -385,12 +397,11 @@ def tile_ambisonicdirectionaldynamicrangecompress_x2_kernel(
                 store_scales(0, 8)
         quant_c(15)
         stage2_planes(15)
-        stage2(15)
-        turn_back(12)
         quant_p(10, 2)
         copy_planes(14)
+        stage2(15)
         quant_p(14, 1)
-        copy_planes(15)
         quant_p(12, 2)
+        copy_planes(15)
         quant_p(15, 1)
         store_scales(8, NT)

@@ -22,13 +22,16 @@ AX = mybir.AxisListType
 
 UNITS = [(0, 128), (128, 128), (256, 256), (512, 512), (1024, 512), (1536, 512)]
 NT = TOKENS // P
-FOLDED = (2, 4, 5, 6, 8, 9, 10, 12, 13)
-TURN = {0: ((2, 0),), 1: ((3, 0), (3, 256)), 3: ((4, 0), (4, 256)), 5: ((5, 0), (5, 256))}
-ON_S = ()
-AFTER = {0: (("prep", 2),), 1: (("prep", 3), ("sum", 0)), 3: (("prep", 4), ("sum", 1)), 4: (("sum", 2), ("sum", 3)), 5: (("prep", 5), ("sum", 4)), 6: (("sum", 5),), 7: (("sum", 7),), 8: (("sum", 6),), 9: (), 10: (("sum", 8),), 11: (("sum", 9), ("sum", 11)), 12: (("sum", 10),), 13: (("sum", 12),), 14: (("sum", 14),), 15: (("sum", 13), ("sum", 15),)}
+FOLDED = ()
+TURN = {0: ((2, 0),), 1: ((3, 0), (3, 256)), 3: ((4, 0), (4, 256)), 6: ((5, 0), (5, 256))}
+ON_S = ((5, 0), (5, 256))
+PREP = {0: 2, 1: 3, 3: 4, 6: 5}
+FLAG = 2
+HOLD = 2
 LAG = 2
 DIRECT = (14, 15)
 ACC = 5
+CAST_G = ()
 
 
 def tile_ambisonicdirectionaldynamicrangecompress_x2_kernel(
@@ -74,12 +77,14 @@ def tile_ambisonicdirectionaldynamicrangecompress_x2_kernel(
 
         def load_x(u):
             tok, width = UNITS[u]
-            nc.sync.dma_start(out=x_tiles[u][:], in_=s_rows[tok : tok + width, :].rearrange("(i p) n -> p i n", p=P))
+            nc.sync.dma_start(out=x_tiles[u][:], in_=s_rows[tok : tok + width, :].rearrange("(p i) n -> p i n", p=P))
 
         load_x(0)
         for q in range(4):
             nc.sync.dma_start(out=ys_raw[32 * q : 32 * q + 4, :].bitcast(I32), in_=ydec_scales[0, 4 * q : 4 * q + 4, :].bitcast(I32))
-        nc.sync.dma_start(out=yd_raw[:].bitcast(I32), in_=ydec_words[0].bitcast(I32))
+        for g in range(2):
+            half = slice(1024 * g, 1024 * (g + 1))
+            nc.sync.dma_start(out=yd_raw[:, half].bitcast(I32), in_=ydec_words[0, :, half].bitcast(I32))
         nc.scalar.dma_start(out=thr_b[:], in_=thr.rearrange("(g p t) -> p g t", g=2, t=4))
         nc.scalar.dma_start(out=w_b[:], in_=w.rearrange("(g p t) -> p g t", g=2, t=4))
         for u in range(1, len(UNITS)):
@@ -129,13 +134,15 @@ def tile_ambisonicdirectionaldynamicrangecompress_x2_kernel(
             xt_tiles[u, b] = xt
 
         def spread(u, b, copy):
+            per = UNITS[u][1] // P
             if b == 0:
                 xg = work.tile([P, 512, 4], BF16, name="xg", align_bytes=64)
                 xg_tiles[u] = xg
-            n = min(256, UNITS[u][1] - b)
+            n = min(256, UNITS[u][1] - b) // P
+            words = xg_tiles[u][:, : UNITS[u][1], :].rearrange("p n t -> p (n t)").bitcast(F32)
             copy(
-                out=xg_tiles[u][:, b : b + n, :].rearrange("p n t -> p (n t)").bitcast(F32).rearrange("p (i r h) -> p i r h", h=2, r=P),
-                in_=xt_tiles.pop((u, b))[:, : n // P].rearrange("p i h r -> p i r h"),
+                out=words.rearrange("p (r i h) -> p r i h", i=per, h=2)[:, :, b // P : b // P + n, :],
+                in_=xt_tiles.pop((u, b))[:, :n].rearrange("p i h r -> p r i h"),
             )
 
         def quant_s(u):
@@ -157,19 +164,19 @@ def tile_ambisonicdirectionaldynamicrangecompress_x2_kernel(
                 stop=True,
             )
 
-        pairs = [(u, k) for u in range(len(UNITS)) for k in range(UNITS[u][1] // P)]
-        N_PAIRS = len(pairs)
+        bank_list = [(0, 0), (1, 0), (0, 4), (1, 4)]
+        for u in range(2, len(UNITS)):
+            bank_list += [(u, d0) for d0 in range(0, 8, 512 // UNITS[u][1])]
+        N_PAIRS = len(bank_list) // 2
         squares = {}
 
         def square(n):
-            u, pair = pairs[n]
-            tok, width = UNITS[u]
-            per_bank = 512 // width
             sq = work.tile([P, 2, 512], F32, name="sq", bufs=8)
             for half in range(2):
+                u, d0 = bank_list[2 * n + half]
+                tok, width = UNITS[u]
                 bank = psum.tile([P, 512], F32, name="acc")
-                d0 = (2 * pair + half) * per_bank
-                for k in range(per_bank):
+                for k in range(512 // width):
                     decode(bank[:, k * width : (k + 1) * width], (d0 + k) // 4, (d0 + k) % 4, tok, width)
                 nc.scalar.activation(out=sq[:, half], in_=bank[:], func=ACT.Square)
             squares[n] = sq
@@ -179,29 +186,20 @@ def tile_ambisonicdirectionaldynamicrangecompress_x2_kernel(
                 nc.gpsimd.tensor_tensor(out=fold[:], in0=v[:, :, 0:8], in1=v[:, :, 8:16], op=ALU.add)
                 squares[n] = fold
 
-        def sums(n):
-            u, pair = pairs[n]
+        def energy_of(n, half):
+            u, d0 = bank_list[2 * n + half]
             tok, width = UNITS[u]
-            per_bank = 512 // width
-            nb = width // SAMPLES
+            return energy[:, d0 : d0 + 512 // width, tok // SAMPLES : (tok + width) // SAMPLES]
+
+        def sums(n):
             t = squares.pop(n)
-            d0 = 2 * pair * per_bank
-            blocks = slice(tok // SAMPLES, tok // SAMPLES + nb)
-            if n in FOLDED:
-                nc.vector.tensor_reduce(
-                    out=energy[:, d0 : d0 + 2 * per_bank, blocks],
-                    in_=t[:].rearrange("p (d b) l -> p d b l", b=nb),
-                    axis=AX.X,
-                    op=ALU.add,
-                )
-            else:
-                for half in range(2):
-                    nc.vector.tensor_reduce(
-                        out=energy[:, d0 + half * per_bank : d0 + (half + 1) * per_bank, blocks],
-                        in_=t[:, half].rearrange("p (d b l) -> p d b l", b=nb, l=SAMPLES),
-                        axis=AX.X,
-                        op=ALU.add,
-                    )
+            for half in range(2):
+                out = energy_of(n, half)
+                nb = out.shape[2]
+                if n in FOLDED:
+                    nc.vector.tensor_reduce(out=out, in_=t[:, 32 * half : 32 * half + 32, :].rearrange("p (d b) l -> p d b l", b=nb), axis=AX.X, op=ALU.add)
+                else:
+                    nc.vector.tensor_reduce(out=out, in_=t[:, half].rearrange("p (d b l) -> p d b l", b=nb, l=SAMPLES), axis=AX.X, op=ALU.add)
 
         def log_gain(b0, b1, k0=0, k1=8):
             for k in range(k0, k1):
@@ -217,20 +215,23 @@ def tile_ambisonicdirectionaldynamicrangecompress_x2_kernel(
         spread(1, 0, on_s)
         quant_s(0)
         permute_ydec(0)
-        permute_ydec(1)
         quant_s(1)
+        permute_ydec(1)
         nc.vector.tensor_scalar(thr16[:], thr_b[:].rearrange("p g t -> p (g t)"), 16.0, None, ALU.mult)
-        for n in range(N_PAIRS):
+        pending = list(range(N_PAIRS))
+        for n in range(N_PAIRS + 4):
             for u, b in TURN.get(n, ()):
                 turn(u, b)
-            square(n)
-            for kind, k in AFTER.get(n, ()):
-                if kind == "prep":
-                    for b in range(0, UNITS[k][1], 256):
-                        spread(k, b, on_s if (k, b) in ON_S else on_v)
-                    quant_s(k)
-                else:
-                    sums(k)
+            if n < N_PAIRS:
+                square(n)
+            if n in PREP:
+                u = PREP[n]
+                for b in range(0, UNITS[u][1], 256):
+                    spread(u, b, on_s if (u, b) in ON_S else on_v)
+                quant_s(u)
+            for k in [k for k in pending if n >= HOLD and k + (FLAG if k in FOLDED else 1) <= n]:
+                sums(k)
+                pending.remove(k)
         log_gain(0, BLOCKS)
         permute_yenc()
 
@@ -312,7 +313,7 @@ def tile_ambisonicdirectionaldynamicrangecompress_x2_kernel(
             turned[i] = og
 
         def stage2(i):
-            cw, cs = ccodes.pop(i)
+            cw, cs = ccodes[i]
             bank = psum.tile([P, CH], F32, name="o", tag="xt", bufs=8 - ACC)
             for g in range(2):
                 nc.tensor.matmul_mx(
@@ -331,6 +332,21 @@ def tile_ambisonicdirectionaldynamicrangecompress_x2_kernel(
                 results[i] = res
 
         def cast(i):
+            if i in CAST_G:
+                rb = work.tile([P, CH], BF16, name="rb", bufs=4)
+                nc.gpsimd.tensor_scalar(
+                    rb[:].rearrange("p (h w e) -> p h w e", h=2, e=2),
+                    results.pop(i)[:].rearrange("p (w h e) -> p h w e", h=2, e=2),
+                    1.0,
+                    0.0,
+                    ALU.mult,
+                    ALU.add,
+                )
+                rounded[i] = rb
+            else:
+                cast_s(i)
+
+        def cast_s(i):
             rb = work.tile([P, CH], BF16, name="rb", bufs=4)
             nc.scalar.copy(
                 out=rb[:].rearrange("p (h w e) -> p h w e", h=2, e=2),
@@ -376,28 +392,23 @@ def tile_ambisonicdirectionaldynamicrangecompress_x2_kernel(
             if i >= 1:
                 quant_c(i - 1)
             apply_gain(i, 1)
-            if i == NT - 1:
-                turn_back(i - 3)
-            if i - 1 in DIRECT:
-                stage2_planes(i - 1)
+            if i - 2 in results:
+                cast(i - 2)
             if i >= 1:
                 stage2(i - 1)
+            if i - 1 in DIRECT:
+                stage2_planes(i - 1)
             for k in range(2):
                 stage1(nxt // 2, nxt % 2)
                 nxt += 1
-            if i - 2 in results:
-                cast(i - 2)
-            if i == NT - 2:
-                cast(i - 1)
-            if i % 2 == 0 and i - 4 in rounded:
-                turn_back(i - 4)
-            if i % 2 == 0 and i - 6 in turned:
-                quant_p(i - 6, 2)
+            if i % 2 == 1 and i - 3 in rounded:
+                turn_back(i - 3)
+            if i % 2 == 1 and i - 5 in turned:
+                quant_p(i - 5, 2)
             if i == 14:
                 store_scales(0, 8)
         quant_c(15)
         stage2_planes(15)
-        quant_p(10, 2)
         copy_planes(14)
         stage2(15)
         quant_p(14, 1)

@@ -22,15 +22,16 @@ AX = mybir.AxisListType
 
 UNITS = [(0, 128), (128, 128), (256, 256), (512, 512), (1024, 512), (1536, 512)]
 NT = TOKENS // P
-FOLDED = ()
-TURN = {0: ((2, 0),), 1: ((3, 0), (3, 256)), 3: ((4, 0), (4, 256)), 6: ((5, 0), (5, 256))}
-ON_S = ((5, 0), (5, 256))
-PREP = {0: 2, 1: 3, 3: 4, 6: 5}
-FLAG = 2
-HOLD = 2
+FOLDED = (2, 4, 6, 7, 8, 10, 12)
+TURN = {0: ((2, 0),), 1: ((3, 0), (3, 256)), 3: ((4, 0), (4, 256)), 5: ((5, 0), (5, 256))}
+ON_S = ((4, 256),)
+PREP = {0: 2, 1: 3, 3: 4, 5: 5}
+FLAG = 3
+HOLD = 1
 LAG = 2
 DIRECT = (14, 15)
 ACC = 5
+TL = 3
 CAST_G = ()
 
 
@@ -293,7 +294,7 @@ def tile_ambisonicdirectionaldynamicrangecompress_x2_kernel(
 
         def stage2_planes(i):
             cw, cs = ccodes[i]
-            bank = psum.tile([P, 4, P], F32, name="o", tag="xt", bufs=8 - ACC)
+            bank = psum.tile([P, 4, P], F32, name="acc")
             for t in range(4):
                 for g in range(2):
                     nc.tensor.matmul_mx(
@@ -401,18 +402,23 @@ def tile_ambisonicdirectionaldynamicrangecompress_x2_kernel(
             for k in range(2):
                 stage1(nxt // 2, nxt % 2)
                 nxt += 1
-            if i % 2 == 1 and i - 3 in rounded:
-                turn_back(i - 3)
-            if i % 2 == 1 and i - 5 in turned:
-                quant_p(i - 5, 2)
+            if i % 2 == 1 and i - TL in rounded and i < 15:
+                turn_back(i - TL)
+            if i % 2 == 1 and i - TL - 2 in turned:
+                quant_p(i - TL - 2, 2)
             if i == 14:
                 store_scales(0, 8)
         quant_c(15)
         stage2_planes(15)
-        copy_planes(14)
         stage2(15)
-        quant_p(14, 1)
-        quant_p(12, 2)
+        if 12 in rounded:
+            turn_back(12)
+        if 10 in turned:
+            quant_p(10, 2)
+        copy_planes(14)
+        store_scales(8, 12)
         copy_planes(15)
+        quant_p(14, 1)
         quant_p(15, 1)
-        store_scales(8, NT)
+        quant_p(12, 2)
+        store_scales(12, NT)

from contextlib import ExitStack

import concourse.mybir as mybir
from concourse.masks import make_identity

TOKENS, CH, DIRS = 2048, 512, 1024
SAMPLES = 16
BLOCKS = TOKENS // SAMPLES
P = 128
FLOPS = 2 * TOKENS * CH * DIRS * 2

F32 = mybir.dt.float32
BF16 = mybir.dt.bfloat16
I32 = mybir.dt.int32
U32 = mybir.dt.uint32
U8 = mybir.dt.uint8
FP8X4 = mybir.dt.float8_e4m3fn_x4
FP4X4 = mybir.dt.float4_e2m1fn_x4
ACT = mybir.ActivationFunctionType
ALU = mybir.AluOpType
AX = mybir.AxisListType

UNITS = [(0, 128), (128, 128), (256, 256), (512, 512), (1024, 512), (1536, 512)]
NT = TOKENS // P
FOLDED = (2, 4, 6, 7, 8, 10, 12)
TURN = {0: ((2, 0),), 1: ((3, 0), (3, 256)), 3: ((4, 0), (4, 256)), 5: ((5, 0), (5, 256))}
ON_S = ((4, 256),)
PREP = {0: 2, 1: 3, 3: 4, 5: 5}
FLAG = 3
HOLD = 1
LAG = 2
DIRECT = (14, 15)
ACC = 5
TL = 3
CAST_G = ()


def tile_ambisonicdirectionaldynamicrangecompress_x2_kernel(
    tc, s, ydec_words, ydec_scales, thr, w, yenc_words, yenc_scales, out_0, out_1, out_2
):
    nc = tc.nc
    s_rows = s.rearrange("j l n -> (j l) n")
    out_rows = out_0.rearrange("j l n -> (j l) n")
    word_rows = out_1[0].rearrange("p m t -> p (m t)").bitcast(I32)
    scale_rows = out_2[0].bitcast(I32)

    with ExitStack() as ctx:
        keep = ctx.enter_context(tc.tile_pool(name="keep", bufs=1))
        work = ctx.enter_context(tc.tile_pool(name="work", bufs=3))
        psum = ctx.enter_context(tc.psum_pool(name="psum", bufs=ACC))
        ctx.enter_context(tc.manual_schedule())

        ident = keep.tile([P, P], F32, name="ident")
        make_identity(nc, ident[:])

        yd_raw = keep.tile([P, 2 * DIRS], U8, name="yd_raw", align_bytes=64)
        ys_raw = keep.tile([P, DIRS], U8, name="ys_raw", align_bytes=64)
        yd = keep.tile([P, 2, 4, P, 2], U8, name="yd", align_bytes=64)
        ys = keep.tile([P, 2, 4, P], U8, name="ys", align_bytes=64)
        ye = keep.tile([P, 2, 2 * CH], U8, name="ye", align_bytes=64)
        yes = keep.tile([P, 2, CH], U8, name="yes", align_bytes=64)
        yp = keep.tile([P, 2, 4, P, 2], U8, name="yp", align_bytes=64)
        yps = keep.tile([P, 2, 4, P], U8, name="yps", align_bytes=64)
        thr_b = keep.tile([P, 2, 4], BF16, name="thr_b")
        w_b = keep.tile([P, 2, 4], BF16, name="w_b")
        thr16 = keep.tile([P, 8], F32, name="thr16")
        lnthr = keep.tile([P, 8], F32, name="lnthr")
        powthr = keep.tile([P, 8], F32, name="powthr")
        wq = keep.tile([P, 2, 4], F32, name="wq")

        nc.vector.memset(ys_raw[:].bitcast(I32), 0)
        nc.vector.memset(yes[:].rearrange("p g n -> p (g n)").bitcast(I32), 0)

        x_tiles = []
        for tok, width in UNITS:
            x = keep.tile([P, width // P, CH], BF16, name="x%d" % tok)
            x_tiles.append(x)

        def load_x(u):
            tok, width = UNITS[u]
            nc.sync.dma_start(out=x_tiles[u][:], in_=s_rows[tok : tok + width, :].rearrange("(p i) n -> p i n", p=P))

        load_x(0)
        for q in range(4):
            nc.sync.dma_start(out=ys_raw[32 * q : 32 * q + 4, :].bitcast(I32), in_=ydec_scales[0, 4 * q : 4 * q + 4, :].bitcast(I32))
        for g in range(2):
            half = slice(1024 * g, 1024 * (g + 1))
            nc.sync.dma_start(out=yd_raw[:, half].bitcast(I32), in_=ydec_words[0, :, half].bitcast(I32))
        nc.scalar.dma_start(out=thr_b[:], in_=thr.rearrange("(g p t) -> p g t", g=2, t=4))
        nc.scalar.dma_start(out=w_b[:], in_=w.rearrange("(g p t) -> p g t", g=2, t=4))
        for u in range(1, len(UNITS)):
            load_x(u)
        nc.sync.dma_start(out=ye[:].rearrange("p g n -> p (g n)").bitcast(I32).rearrange("p (g n) -> p g n", g=2), in_=yenc_words.rearrange("g p n -> p g n").bitcast(I32))
        for q in range(4):
            nc.sync.dma_start(
                out=yes[32 * q : 32 * q + 4, :, :].rearrange("p g n -> p (g n)").bitcast(I32).rearrange("p (g n) -> p g n", g=2),
                in_=yenc_scales[:, 4 * q : 4 * q + 4, :].rearrange("g q n -> q g n").bitcast(I32),
            )

        nc.scalar.activation(out=lnthr[:], in_=thr_b[:].rearrange("p g t -> p (g t)"), func=ACT.Ln, scale=16.0)

        s_codes = keep.tile([P, TOKENS], U32, name="s_codes", align_bytes=64)
        s_scales = keep.tile([P, TOKENS], U8, name="s_scales", align_bytes=64)
        energy = keep.tile([P, 8, BLOCKS], F32, name="energy")
        lnsum = keep.tile([P, 8, BLOCKS], F32, name="lnsum")
        power = keep.tile([P, 8, BLOCKS], F32, name="power")
        gain = keep.tile([P, 2, BLOCKS, 4], F32, name="gain")

        def permute_ydec(g):
            nc.vector.tensor_copy(
                out=yd[:, g],
                in_=yd_raw[:, 1024 * g : 1024 * (g + 1)].rearrange("p (m t b) -> p t m b", t=4, b=2),
            )
            nc.vector.tensor_copy(
                out=ys[:, g],
                in_=ys_raw[:, 512 * g : 512 * (g + 1)].rearrange("p (m t) -> p t m", t=4),
            )

        def permute_yenc():
            for g in range(2):
                nc.vector.tensor_copy(out=yp[:, g], in_=ye[:, g].rearrange("p (m t b) -> p t m b", t=4, b=2))
            nc.vector.tensor_copy(out=yps[:], in_=yes[:].rearrange("p g (m t) -> p g t m", t=4))

        xg_tiles = {}

        xt_tiles = {}

        def turn(u, b):
            n = min(256, UNITS[u][1] - b)
            xt = psum.tile([P, 2, 2, P], F32, name="xt", bufs=8 - ACC)
            for i in range(n // P):
                words = x_tiles[u][:, b // P + i, :].bitcast(F32)
                for h in range(2):
                    nc.tensor.transpose(xt[:, i, h, :], words[:, h::2], ident[:])
            xt_tiles[u, b] = xt

        def spread(u, b, copy):
            per = UNITS[u][1] // P
            if b == 0:
                xg = work.tile([P, 512, 4], BF16, name="xg", align_bytes=64)
                xg_tiles[u] = xg
            n = min(256, UNITS[u][1] - b) // P
            words = xg_tiles[u][:, : UNITS[u][1], :].rearrange("p n t -> p (n t)").bitcast(F32)
            copy(
                out=words.rearrange("p (r i h) -> p r i h", i=per, h=2)[:, :, b // P : b // P + n, :],
                in_=xt_tiles.pop((u, b))[:, :n].rearrange("p i h r -> p r i h"),
            )

        def quant_s(u):
            tok, width = UNITS[u]
            nc.vector.quantize_mx(
                out=s_codes[:, tok : tok + width].bitcast(FP8X4),
                scales=s_scales[:, tok : tok + width],
                in_=xg_tiles.pop(u)[:, :width, :].rearrange("p n t -> p (n t)"),
            )

        def decode(out, g, t, tok, width):
            nc.tensor.matmul_mx(
                out=out,
                lhsT=yd[:, g, t].rearrange("p m b -> p (m b)").bitcast(FP4X4),
                lhsT_scale=ys[:, g, t],
                rhs=s_codes[:, tok : tok + width].bitcast(FP8X4),
                rhs_scale=s_scales[:, tok : tok + width],
                start=True,
                stop=True,
            )

        bank_list = [(0, 0), (1, 0), (0, 4), (1, 4)]
        for u in range(2, len(UNITS)):
            bank_list += [(u, d0) for d0 in range(0, 8, 512 // UNITS[u][1])]
        N_PAIRS = len(bank_list) // 2
        squares = {}

        def square(n):
            sq = work.tile([P, 2, 512], F32, name="sq", bufs=8)
            for half in range(2):
                u, d0 = bank_list[2 * n + half]
                tok, width = UNITS[u]
                bank = psum.tile([P, 512], F32, name="acc")
                for k in range(512 // width):
                    decode(bank[:, k * width : (k + 1) * width], (d0 + k) // 4, (d0 + k) % 4, tok, width)
                nc.scalar.activation(out=sq[:, half], in_=bank[:], func=ACT.Square)
            squares[n] = sq
            if n in FOLDED:
                fold = work.tile([P, 64, 8], F32, name="fold", bufs=6)
                v = sq[:].rearrange("p h (b l) -> p (h b) l", l=SAMPLES)
                nc.gpsimd.tensor_tensor(out=fold[:], in0=v[:, :, 0:8], in1=v[:, :, 8:16], op=ALU.add)
                squares[n] = fold

        def energy_of(n, half):
            u, d0 = bank_list[2 * n + half]
            tok, width = UNITS[u]
            return energy[:, d0 : d0 + 512 // width, tok // SAMPLES : (tok + width) // SAMPLES]

        def sums(n):
            t = squares.pop(n)
            for half in range(2):
                out = energy_of(n, half)
                nb = out.shape[2]
                if n in FOLDED:
                    nc.vector.tensor_reduce(out=out, in_=t[:, 32 * half : 32 * half + 32, :].rearrange("p (d b) l -> p d b l", b=nb), axis=AX.X, op=ALU.add)
                else:
                    nc.vector.tensor_reduce(out=out, in_=t[:, half].rearrange("p (d b l) -> p d b l", b=nb, l=SAMPLES), axis=AX.X, op=ALU.add)

        def log_gain(b0, b1, k0=0, k1=8):
            for k in range(k0, k1):
                nc.scalar.activation(out=lnsum[:, k, b0:b1], in_=energy[:, k, b0:b1], func=ACT.Ln, bias=thr16[:, k : k + 1])

        on_v = nc.vector.tensor_copy
        on_s = nc.scalar.copy
        on_v = nc.vector.tensor_copy
        on_s = nc.scalar.copy
        turn(0, 0)
        turn(1, 0)
        spread(0, 0, on_v)
        spread(1, 0, on_s)
        quant_s(0)
        permute_ydec(0)
        quant_s(1)
        permute_ydec(1)
        nc.vector.tensor_scalar(thr16[:], thr_b[:].rearrange("p g t -> p (g t)"), 16.0, None, ALU.mult)
        pending = list(range(N_PAIRS))
        for n in range(N_PAIRS + 4):
            for u, b in TURN.get(n, ()):
                turn(u, b)
            if n < N_PAIRS:
                square(n)
            if n in PREP:
                u = PREP[n]
                for b in range(0, UNITS[u][1], 256):
                    spread(u, b, on_s if (u, b) in ON_S else on_v)
                quant_s(u)
            for k in [k for k in pending if n >= HOLD and k + (FLAG if k in FOLDED else 1) <= n]:
                sums(k)
                pending.remove(k)
        log_gain(0, BLOCKS)
        permute_yenc()

        def finish_gain(b0, b1, first):
            nc.scalar.activation(out=power[:, :, b0:b1], in_=lnsum[:, :, b0:b1], func=ACT.Exp, scale=-0.35)
            eng = nc.vector if first else nc.gpsimd
            eng.tensor_tensor(
                out=gain[:, :, b0:b1, :],
                in0=power[:, :, b0:b1].rearrange("p (g t) b -> p g b t", g=2),
                in1=wq[:].unsqueeze(2).to_broadcast([P, 2, b1 - b0, 4]),
                op=ALU.mult,
            )

        nc.scalar.activation(out=powthr[:], in_=lnthr[:], func=ACT.Exp, scale=0.35)
        nc.vector.tensor_tensor(out=wq[:].rearrange("p g t -> p (g t)"), in0=powthr[:], in1=w_b[:].rearrange("p g t -> p (g t)"), op=ALU.mult)
        finish_gain(0, 8, True)
        finish_gain(8, 32, False)
        finish_gain(32, 80, False)
        finish_gain(80, 128, False)

        p_codes = keep.tile([P, TOKENS], U32, name="p_codes", align_bytes=64)
        p_scales = keep.tile([P, TOKENS], U8, name="p_scales", align_bytes=64)
        banks = {}
        comp = {}
        ccodes = {}
        rounded = {}
        turned = {}
        direct = {}
        results = {}

        def stage1(i, g):
            if i >= NT:
                return
            bank = psum.tile([P, 4, P], F32, name="acc")
            for t in range(4):
                decode(bank[:, t], g, t, P * i, P)
            banks[i, g] = bank

        def apply_gain(i, g):
            if g == 0:
                c = work.tile([P, 2, P, 4], BF16, name="c", align_bytes=64)
                comp[i] = c
            nc.vector.tensor_tensor(
                out=comp[i][:, g].rearrange("p (b l) t -> p b l t", l=SAMPLES),
                in0=banks.pop((i, g))[:].rearrange("p t (b l) -> p b l t", l=SAMPLES),
                in1=gain[:, g, 8 * i : 8 * i + 8, :].unsqueeze(2).to_broadcast([P, 8, SAMPLES, 4]),
                op=ALU.mult,
            )

        def quant_c(i):
            cw = work.tile([P, 2, P], U32, name="cw", align_bytes=64)
            cs = work.tile([P, 2, P], U8, name="cs", align_bytes=64)
            nc.vector.quantize_mx(
                out=cw[:].rearrange("p g n -> p (g n)").bitcast(FP8X4),
                scales=cs[:].rearrange("p g n -> p (g n)"),
                in_=comp.pop(i)[:].rearrange("p g n t -> p (g n t)"),
            )
            ccodes[i] = (cw, cs)

        def stage2_planes(i):
            cw, cs = ccodes[i]
            bank = psum.tile([P, 4, P], F32, name="acc")
            for t in range(4):
                for g in range(2):
                    nc.tensor.matmul_mx(
                        out=bank[:, t],
                        lhsT=yp[:, g, t].rearrange("p m b -> p (m b)").bitcast(FP4X4),
                        lhsT_scale=yps[:, g, t],
                        rhs=cw[:, g].bitcast(FP8X4),
                        rhs_scale=cs[:, g],
                        start=g == 0,
                        stop=g == 1,
                    )
            direct[i] = bank

        def copy_planes(i):
            og = work.tile([P, 2 * P, 4], BF16, name="og", align_bytes=64)
            nc.vector.tensor_copy(out=og[:, :P], in_=direct.pop(i)[:].rearrange("p t r -> p r t"))
            turned[i] = og

        def stage2(i):
            cw, cs = ccodes[i]
            bank = psum.tile([P, CH], F32, name="o", tag="xt", bufs=8 - ACC)
            for g in range(2):
                nc.tensor.matmul_mx(
                    out=bank[:],
                    lhsT=cw[:, g].bitcast(FP8X4),
                    lhsT_scale=cs[:, g],
                    rhs=ye[:, g].bitcast(FP4X4),
                    rhs_scale=yes[:, g],
                    start=g == 0,
                    stop=g == 1,
                )
            res = work.tile([P, CH], F32, name="res", bufs=4)
            nc.scalar.copy(out=res[:], in_=bank[:])
            nc.sync.dma_start(out=out_rows[P * i : P * (i + 1), :], in_=res[:])
            if i not in DIRECT:
                results[i] = res

        def cast(i):
            if i in CAST_G:
                rb = work.tile([P, CH], BF16, name="rb", bufs=4)
                nc.gpsimd.tensor_scalar(
                    rb[:].rearrange("p (h w e) -> p h w e", h=2, e=2),
                    results.pop(i)[:].rearrange("p (w h e) -> p h w e", h=2, e=2),
                    1.0,
                    0.0,
                    ALU.mult,
                    ALU.add,
                )
                rounded[i] = rb
            else:
                cast_s(i)

        def cast_s(i):
            rb = work.tile([P, CH], BF16, name="rb", bufs=4)
            nc.scalar.copy(
                out=rb[:].rearrange("p (h w e) -> p h w e", h=2, e=2),
                in_=results.pop(i)[:].rearrange("p (w h e) -> p h w e", h=2, e=2),
            )
            rounded[i] = rb

        def turn_back(i):
            xt = psum.tile([P, 2, 2, P], F32, name="xt", bufs=8 - ACC)
            for k in range(2):
                words = rounded.pop(i + k)[:].bitcast(F32)
                for h in range(2):
                    nc.tensor.transpose(xt[:, k, h, :], words[:, P * h : P * (h + 1)], ident[:])
            og = work.tile([P, 2 * P, 4], BF16, name="og", align_bytes=64)
            nc.scalar.copy(
                out=og[:].rearrange("p n t -> p (n t)").bitcast(F32).rearrange("p (i r h) -> p i r h", h=2, r=P),
                in_=xt[:].rearrange("p i h r -> p i r h"),
            )
            turned[i] = og

        def quant_p(i, n):
            cols = slice(P * i, P * (i + n))
            nc.vector.quantize_mx(
                out=p_codes[:, cols].bitcast(FP8X4),
                scales=p_scales[:, cols],
                in_=turned.pop(i)[:, : n * P].rearrange("p n t -> p (n t)"),
            )
            nc.sync.dma_start(out=word_rows[:, cols], in_=p_codes[:, cols].bitcast(I32))

        def store_scales(i0, i1):
            words = slice(i0 * P // 4, i1 * P // 4)
            for q in range(4):
                (nc.scalar if q % 2 else nc.sync).dma_start(
                    out=scale_rows[4 * q : 4 * q + 4, words],
                    in_=p_scales[32 * q : 32 * q + 4, :].bitcast(I32)[:, words],
                )

        for k in range(ACC):
            stage1(k // 2, k % 2)
        nxt = ACC
        for i in range(NT):
            apply_gain(i, 0)
            if i >= 1:
                quant_c(i - 1)
            apply_gain(i, 1)
            if i - 2 in results:
                cast(i - 2)
            if i >= 1:
                stage2(i - 1)
            if i - 1 in DIRECT:
                stage2_planes(i - 1)
            for k in range(2):
                stage1(nxt // 2, nxt % 2)
                nxt += 1
            if i % 2 == 1 and i - TL in rounded and i < 15:
                turn_back(i - TL)
            if i % 2 == 1 and i - TL - 2 in turned:
                quant_p(i - TL - 2, 2)
            if i == 14:
                store_scales(0, 8)
        quant_c(15)
        stage2_planes(15)
        stage2(15)
        if 12 in rounded:
            turn_back(12)
        if 10 in turned:
            quant_p(10, 2)
        copy_planes(14)
        store_scales(8, 12)
        copy_planes(15)
        quant_p(14, 1)
        quant_p(15, 1)
        quant_p(12, 2)
        store_scales(12, NT)
